import numpy as np
CORES = [4,5,6,7,12,13,14,15,132,133,134,135,140,141,142,143]
N = 16
GROUPS = [[0,1,2,3],[4,5,6,7],[8,9,10,11],[12,13,14,15]]
def setup_inputs(rng):
    return {"x": rng.standard_normal((N, 128, 2048), dtype=np.float32)}
def reference(x):
    y = np.empty((N, 128, 2048), x.dtype)
    for g in GROUPS:
        n = len(g); b = x.shape[2] // n
        for i, r in enumerate(g):
            y[r] = np.concatenate([x[s][:, i * b:(i + 1) * b] for s in g], axis=1)
    return {"y": y}

@@ -1,0 +1,58 @@
+from concourse.bass import DstId, RemoteDMATransfer
+
+B = 512
+SCRATCH = {
+    "stage": ("sbuf", [128, 3 * B], "float32"),
+    "land": ("sbuf", [128, 3 * B], "float32"),
+}
+SEMAPHORES = ["ld12", "ld3", "arr1", "arr2", "arr3", "sent", "stored"]
+
+
+def rank_program(g, core, T, topo):
+    rank = T.rank_of(core)
+    if rank is None:
+        return
+    grp = [gr for gr in T.tables["GROUPS"] if rank in gr][0]
+    n = len(grp)
+    i = grp.index(rank)
+    b = T.x.shape[1] // n
+    s = T.sem
+
+    def blk(t, j):
+        return t[:, j * b:(j + 1) * b]
+
+    def to(k):
+        return (i + k) % n
+
+    def address(k):
+        return topo.addr(T.cores[grp[to(k)]], core)
+
+    def dst_id(k):
+        rid, pid = address(k)
+        return DstId(rid=rid, pnc=pid)
+
+    g.sync.dma_start(blk(T.stage, 0), blk(T.x, to(1))).then_inc(s.ld12, 16)
+    g.scalar.dma_start(blk(T.stage, 1), blk(T.x, to(2))).then_inc(s.ld12, 16)
+    g.sync.dma_start(blk(T.stage, 2), blk(T.x, to(3))).then_inc(s.ld3, 16)
+    g.scalar.dma_start(blk(T.y, i), blk(T.x, i)).then_inc(s.stored, 16)
+
+    g.wait_ge(s.ld12, 32)
+    g.remote_dma_fused([
+        RemoteDMATransfer(dst_ids=[dst_id(1)], dma_engine_mask=0x00FF, remote_sem=s.arr1,
+                          src=blk(T.stage, 0), dst=blk(T.land, 0)),
+        RemoteDMATransfer(dst_ids=[dst_id(2)], dma_engine_mask=0xFF00, remote_sem=s.arr2,
+                          src=blk(T.stage, 1), dst=blk(T.land, 1)),
+    ], local_sem=s.sent)
+    g.wait_ge(s.ld3, 16)
+    rid3, pid3 = address(3)
+    g.remote_dma(blk(T.land, 2), blk(T.stage, 2), s.arr3, s.sent, pid3, rid3, 0xFFFF)
+
+    g.sync.wait_ge(s.arr1, 8)
+    g.sync.dma_start(blk(T.y, to(-1)), blk(T.land, 0)).then_inc(s.stored, 16)
+    g.scalar.wait_ge(s.arr2, 8)
+    g.scalar.dma_start(blk(T.y, to(-2)), blk(T.land, 1)).then_inc(s.stored, 16)
+    g.sync.wait_ge(s.arr3, 16)
+    g.sync.dma_start(blk(T.y, to(-3)), blk(T.land, 2)).then_inc(s.stored, 16)
+
+    g.wait_ge(s.sent, 32)
+    g.wait_ge(s.stored, 64)

@@ -1,11 +1,9 @@
-from concourse.bass import DstId, RemoteDMATransfer
-
 B = 512
 SCRATCH = {
     "stage": ("sbuf", [128, 3 * B], "float32"),
     "land": ("sbuf", [128, 3 * B], "float32"),
 }
-SEMAPHORES = ["ld12", "ld3", "arr1", "arr2", "arr3", "sent", "stored"]
+SEMAPHORES = ["ld1", "ld2", "ld3", "arr1", "arr2", "arr3", "sent", "stored"]
 
 
 def rank_program(g, core, T, topo):
@@ -24,35 +22,24 @@ def rank_program(g, core, T, topo):
     def to(k):
         return (i + k) % n
 
-    def address(k):
-        return topo.addr(T.cores[grp[to(k)]], core)
-
-    def dst_id(k):
-        rid, pid = address(k)
-        return DstId(rid=rid, pnc=pid)
-
-    g.sync.dma_start(blk(T.stage, 0), blk(T.x, to(1))).then_inc(s.ld12, 16)
-    g.scalar.dma_start(blk(T.stage, 1), blk(T.x, to(2))).then_inc(s.ld12, 16)
+    g.sync.dma_start(blk(T.stage, 0), blk(T.x, to(1))).then_inc(s.ld1, 16)
+    g.scalar.dma_start(blk(T.stage, 1), blk(T.x, to(2))).then_inc(s.ld2, 16)
     g.sync.dma_start(blk(T.stage, 2), blk(T.x, to(3))).then_inc(s.ld3, 16)
+
+    for k in (1, 2, 3):
+        rid, pid = topo.addr(T.cores[grp[to(k)]], core)
+        g.wait_ge(s["ld%d" % k], 16)
+        g.remote_dma(blk(T.land, k - 1), blk(T.stage, k - 1), s["arr%d" % k], s.sent, pid, rid, 0xFFFF)
+
+    g.scalar.wait_ge(s.ld3, 16)
     g.scalar.dma_start(blk(T.y, i), blk(T.x, i)).then_inc(s.stored, 16)
 
-    g.wait_ge(s.ld12, 32)
-    g.remote_dma_fused([
-        RemoteDMATransfer(dst_ids=[dst_id(1)], dma_engine_mask=0x00FF, remote_sem=s.arr1,
-                          src=blk(T.stage, 0), dst=blk(T.land, 0)),
-        RemoteDMATransfer(dst_ids=[dst_id(2)], dma_engine_mask=0xFF00, remote_sem=s.arr2,
-                          src=blk(T.stage, 1), dst=blk(T.land, 1)),
-    ], local_sem=s.sent)
-    g.wait_ge(s.ld3, 16)
-    rid3, pid3 = address(3)
-    g.remote_dma(blk(T.land, 2), blk(T.stage, 2), s.arr3, s.sent, pid3, rid3, 0xFFFF)
-
-    g.sync.wait_ge(s.arr1, 8)
+    g.sync.wait_ge(s.arr1, 16)
     g.sync.dma_start(blk(T.y, to(-1)), blk(T.land, 0)).then_inc(s.stored, 16)
-    g.scalar.wait_ge(s.arr2, 8)
+    g.scalar.wait_ge(s.arr2, 16)
     g.scalar.dma_start(blk(T.y, to(-2)), blk(T.land, 1)).then_inc(s.stored, 16)
     g.sync.wait_ge(s.arr3, 16)
     g.sync.dma_start(blk(T.y, to(-3)), blk(T.land, 2)).then_inc(s.stored, 16)
 
-    g.wait_ge(s.sent, 32)
+    g.wait_ge(s.sent, 48)
     g.wait_ge(s.stored, 64)

B = 512
SCRATCH = {
    "stage": ("sbuf", [128, 3 * B], "float32"),
    "land": ("sbuf", [128, 3 * B], "float32"),
}
SEMAPHORES = ["ld1", "ld2", "ld3", "arr1", "arr2", "arr3", "sent", "stored"]


def rank_program(g, core, T, topo):
    rank = T.rank_of(core)
    if rank is None:
        return
    grp = [gr for gr in T.tables["GROUPS"] if rank in gr][0]
    n = len(grp)
    i = grp.index(rank)
    b = T.x.shape[1] // n
    s = T.sem

    def blk(t, j):
        return t[:, j * b:(j + 1) * b]

    def to(k):
        return (i + k) % n

    g.sync.dma_start(blk(T.stage, 0), blk(T.x, to(1))).then_inc(s.ld1, 16)
    g.scalar.dma_start(blk(T.stage, 1), blk(T.x, to(2))).then_inc(s.ld2, 16)
    g.sync.dma_start(blk(T.stage, 2), blk(T.x, to(3))).then_inc(s.ld3, 16)

    for k in (1, 2, 3):
        rid, pid = topo.addr(T.cores[grp[to(k)]], core)
        g.wait_ge(s["ld%d" % k], 16)
        g.remote_dma(blk(T.land, k - 1), blk(T.stage, k - 1), s["arr%d" % k], s.sent, pid, rid, 0xFFFF)

    g.scalar.wait_ge(s.ld3, 16)
    g.scalar.dma_start(blk(T.y, i), blk(T.x, i)).then_inc(s.stored, 16)

    g.sync.wait_ge(s.arr1, 16)
    g.sync.dma_start(blk(T.y, to(-1)), blk(T.land, 0)).then_inc(s.stored, 16)
    g.scalar.wait_ge(s.arr2, 16)
    g.scalar.dma_start(blk(T.y, to(-2)), blk(T.land, 1)).then_inc(s.stored, 16)
    g.sync.wait_ge(s.arr3, 16)
    g.sync.dma_start(blk(T.y, to(-3)), blk(T.land, 2)).then_inc(s.stored, 16)

    g.wait_ge(s.sent, 48)
    g.wait_ge(s.stored, 64)
